import numpy as np
import ml_dtypes


def mxq(x, axis, fmt="e4m3"):
    dtype, down = {"e4m3": (ml_dtypes.float8_e4m3fn, 7), "e5m2": (ml_dtypes.float8_e5m2, 14)}[fmt]
    v = np.moveaxis(np.asarray(x, np.float32).astype(ml_dtypes.bfloat16).astype(np.float64), axis, -1)
    blocks = v.reshape(v.shape[:-1] + (-1, 32))
    amax = np.abs(blocks).max(-1, keepdims=True)
    byte = np.maximum(np.where(amax > 0, np.frexp(amax)[1] - 1 + 127, 0) - down, 1)
    scale = np.exp2(byte - 127.0)
    codes = (blocks / scale).astype(np.float32).astype(dtype).astype(np.float64)
    return np.moveaxis((codes * scale).reshape(v.shape), -1, axis)


WIDE = False


def mx_kscale(k):
    if not WIDE:
        return np.ones(k)
    levels = np.array([10, -10, 5, -5, 0])
    if k % 512:
        return np.exp2(np.random.permutation(np.resize(levels, k // 32))).repeat(32)
    a = np.empty((k // 512, 16))
    for p in range(k // 512):
        a[p, :8] = np.random.permutation(np.resize(levels, 8))
        for g in range(8):
            far = levels[np.abs(levels - a[p, g]) >= 10]
            a[p, g + 8] = far[np.random.randint(len(far))]
    return np.exp2(a.ravel()).repeat(32)


def f64(x):
    return np.asarray(x).astype(np.float64)


def striped(idx):
    return np.tile(idx.reshape(-1, 16).T, (8, 1)).astype(np.uint16)


def unstriped(offs):
    return offs[:16].T.reshape(-1).astype(np.int64)


E2M1 = np.array([0.0, 0.5, 1.0, 1.5, 2.0, 3.0, 4.0, 6.0, -0.0, -0.5, -1.0, -1.5, -2.0, -3.0, -4.0, -6.0])


def pack_weight(w, fmt):
    k, n = w.shape
    w = f64(np.asarray(w, np.float32).astype(ml_dtypes.bfloat16)).reshape(k // 32, 32, n)
    amax = np.abs(w).max(1)
    if fmt == "e4m3":
        byte = np.frexp(amax)[1] - 1 + 127 - 7
    else:
        mant, ex = np.frexp(amax / 6.0)
        byte = np.where(mant > 0.5, ex, ex - 1) + 127
    byte = np.clip(np.where(amax > 0, byte, 1), 1, 254)
    scaled = (w * np.exp2(127.0 - byte)[:, None, :]).reshape(k, n).astype(np.float32)
    by_word = np.ascontiguousarray(scaled.reshape(k // 512, 128, 4, n).transpose(0, 1, 3, 2))
    if fmt == "e4m3":
        words = by_word.astype(ml_dtypes.float8_e4m3fn).view(np.uint8)
    else:
        c = by_word.astype(ml_dtypes.float4_e2m1fn).view(np.uint8) & 0xF
        words = (c[..., 0::2] | (c[..., 1::2] << 4)).reshape(k // 512, 128, 2 * n)
    return np.ascontiguousarray(words), np.ascontiguousarray(byte.astype(np.uint8).reshape(k // 512, 16, n))


def unpack_weight(words, scales, fmt):
    g, _, n = scales.shape
    words = np.ascontiguousarray(words).reshape(g, 128, n, -1)
    if fmt == "e4m3":
        vals = words.view(ml_dtypes.float8_e4m3fn).astype(np.float64)
    else:
        nib = np.empty((g, 128, n, 4), np.uint8)
        nib[..., 0::2] = words & 0xF
        nib[..., 1::2] = words >> 4
        vals = E2M1[nib]
    vals = vals * np.repeat(np.exp2(scales.astype(np.float64) - 127.0), 8, axis=1)[..., None]
    return vals.transpose(0, 1, 3, 2).reshape(g * 512, n)


def gelu(v):
    return 0.5 * v * (1.0 + np.tanh(np.sqrt(2.0 / np.pi) * (v + 0.044715 * v**3)))


def bf(x):
    return np.asarray(x, np.float32).astype(ml_dtypes.bfloat16)


def planes(Y):
    n, m = Y.shape
    b = f64(bf(Y)).reshape(n // 32, 32, m)
    amax = np.abs(b).max(1)
    byte = np.clip(np.where(amax > 0, np.frexp(amax)[1] - 1 + 127 - 7, 1), 1, 254)
    codes = (b * np.exp2(127.0 - byte)[:, None, :]).reshape(n, m).astype(np.float32).astype(ml_dtypes.float8_e4m3fn).view(np.uint8)
    words = codes.reshape(n // 512, 128, 4, m).transpose(0, 1, 3, 2)
    return np.ascontiguousarray(words), np.ascontiguousarray(byte.astype(np.uint8).reshape(n // 512, 16, m))


K, T, S, P, H, N = 1536, 2048, 1024, 512, 1024, 1024

def setup_inputs():
    n = np.random.standard_normal
    s = mx_kscale(K)[:, None]
    u = mx_kscale(H)[:, None]
    tab_words, tab_scales = pack_weight(n((K, T)) * s, "e4m3")
    w4_words, w4_scales = pack_weight(n((H, N)) / np.sqrt(H) / u, "e2m1")
    return {
        "tab_words": tab_words, "tab_scales": tab_scales,
        "offs": striped(np.random.permutation(T)[:S]),
        "pos1": striped(np.random.permutation(S)[:P]),
        "pos2": striped(np.random.permutation(S)[:P]),
        "w1": (0.72 * n((K, H)) / np.sqrt(K) / s).astype(np.float32),
        "kick": np.random.uniform(3.0, 7.0, H).astype(np.float32),
        "surf": (n((H, P)) * u).astype(np.float32),
        "w4_words": w4_words, "w4_scales": w4_scales,
        "span": (0.6 * np.exp(0.8 * n(N))).astype(np.float32),
    }

def reference(tab_words, tab_scales, offs, pos1, pos2, w1, kick, surf, w4_words, w4_scales, span):
    v = unpack_weight(tab_words, tab_scales, "e4m3")[:, unstriped(offs)]
    h = mxq(f64(w1), 0, "e4m3").T @ v
    top = h.max(axis=1)
    a = np.exp(h[:, unstriped(pos1)] - top[:, None])
    b = f64(kick)[:, None] * a
    d = (b - h[:, unstriped(pos2)]) * f64(surf)
    w4 = unpack_weight(w4_words, w4_scales, "e2m1")
    o = w4.T @ mxq(d, 0, "e4m3")
    y = f64(span)[:, None] * (o + b)
    words, scales = planes(y)
    return y, words, scales

@@ -1,0 +1,274 @@
+from contextlib import ExitStack
+
+import concourse.mybir as mybir
+
+K, T, S, M, H, N = 1536, 2048, 1024, 512, 1024, 1024
+FLOPS = 2 * K * H * S + 2 * H * N * M
+
+F32 = mybir.dt.float32
+BF16 = mybir.dt.bfloat16
+I32 = mybir.dt.int32
+U32 = mybir.dt.uint32
+U16 = mybir.dt.uint16
+U8 = mybir.dt.uint8
+FP8X4 = mybir.dt.float8_e4m3fn_x4
+FP4X4 = mybir.dt.float4_e2m1fn_x4
+ALU = mybir.AluOpType
+ACT = mybir.ActivationFunctionType
+
+P = 128
+PACK = 4
+GROUP = P * PACK
+PASSES = K // GROUP
+GROUPS = H // GROUP
+BANK = 512
+
+
+def tile_list_stride_asymmetry_features_kernel(
+    tc, tab_words, tab_scales, offs, pos1, pos2, w1, kick, surf, w4_words, w4_scales, span, out_0, out_1, out_2
+):
+    nc = tc.nc
+    with ExitStack() as ctx:
+        keep = ctx.enter_context(tc.tile_pool(name="keep", bufs=1))
+        ring = ctx.enter_context(tc.tile_pool(name="ring", bufs=1))
+        psum = ctx.enter_context(tc.psum_pool(name="psum", bufs=1))
+
+        offs_sb = keep.tile([P, S // 16], U16, name="offs_sb")
+        pos1_sb = keep.tile([P, M // 16], U16, name="pos1_sb")
+        pos2_sb = keep.tile([P, M // 16], U16, name="pos2_sb")
+        tabw = [keep.tile([P, T], U32, name=f"tabw{a}", align_bytes=64) for a in range(PASSES)]
+        tabs = keep.tile([P, T], U8, name="tabs", align_bytes=64)
+        vw = [keep.tile([P, S], U32, name=f"vw{a}", align_bytes=64) for a in range(PASSES)]
+        vs = keep.tile([P, S], U8, name="vs", align_bytes=64)
+        w4s_raw = keep.tile([P, GROUPS, N], U8, name="w4s_raw", align_bytes=64)
+        w4s = keep.tile([P, GROUPS, N], U8, name="w4s", align_bytes=64)
+        w4w_raw = keep.tile([P, GROUPS, N], U16, name="w4w_raw", align_bytes=64)
+        w4w = keep.tile([P, GROUPS, N], U16, name="w4w", align_bytes=64)
+        kick_sb = keep.tile([P, GROUPS, 8], F32, name="kick_sb")
+        span_sb = keep.tile([P, GROUPS, 8], F32, name="span_sb")
+        gain = keep.tile([P, GROUPS, 8], F32, name="gain")
+        surf_sb = [keep.tile([P, PACK, M], F32, name=f"surf{b}") for b in range(GROUPS)]
+        diff = [keep.tile([P, PACK, M], F32, name=f"diff{b}") for b in range(GROUPS)]
+        y = [keep.tile([P, PACK, M], F32, name=f"y{b}") for b in range(GROUPS)]
+        d_codes = [keep.tile([P, M], U32, name=f"d_codes{b}", align_bytes=64) for b in range(GROUPS)]
+        d_scales = [keep.tile([P, M], U8, name=f"d_scales{b}", align_bytes=64) for b in range(GROUPS)]
+        y_codes = [keep.tile([P, M], U32, name=f"y_codes{b}", align_bytes=64) for b in range(GROUPS)]
+        y_scales = keep.tile([P, GROUPS, M], U8, name="y_scales", align_bytes=64)
+        look = {}
+        raw, w1c, w1s, banks = {}, {}, {}, {}
+
+        def load_tab(a):
+            nc.sync.dma_start(out=tabw[a][:].bitcast(I32), in_=tab_words[a].rearrange("p n i -> p (n i)").bitcast(I32))
+
+        def load_w1(b, a):
+            raw[b, a] = ring.tile([P, PACK, GROUP], F32, name="w1_raw", bufs=4)
+            rows = w1[a * GROUP : (a + 1) * GROUP, b * GROUP : (b + 1) * GROUP]
+            nc.sync.dma_start(out=raw[b, a][:], in_=rows.rearrange("(p j) c -> p j c", j=PACK))
+
+        def load_surf(b):
+            nc.sync.dma_start(
+                out=surf_sb[b][:], in_=surf[b * GROUP : (b + 1) * GROUP, :].rearrange("(p i) m -> p i m", i=PACK)
+            )
+
+        def quant_w1(b, a, on_vector):
+            grouped = ring.tile([P, PACK, P, PACK], BF16, name="w1_bf", bufs=3, align_bytes=64)
+            dst = grouped[:].rearrange("p t m j -> p m j t")
+            src = raw[b, a][:].rearrange("p j (m t) -> p m j t", t=PACK)
+            if on_vector < P:
+                nc.scalar.copy(out=dst[:, on_vector:P], in_=src[:, on_vector:P])
+            if on_vector > 0:
+                nc.vector.tensor_copy(out=dst[:, 0:on_vector], in_=src[:, 0:on_vector])
+            w1c[b, a] = keep.tile([P, GROUP], U32, name=f"w1c{b}{a}", align_bytes=64)
+            w1s[b, a] = keep.tile([P, GROUP], U8, name=f"w1s{b}{a}", align_bytes=64)
+            nc.vector.quantize_mx(
+                out=w1c[b, a][:].bitcast(FP8X4), scales=w1s[b, a][:], in_=grouped[:].rearrange("p t m j -> p (t m j)")
+            )
+
+        def first_product(b, a):
+            for t in range(PACK):
+                for s in range(2):
+                    if a == 0:
+                        banks[b, t, s] = psum.tile([P, BANK], F32, name=f"bank{2 * t + s}")
+                    nc.tensor.matmul_mx(
+                        out=banks[b, t, s][:],
+                        lhsT=w1c[b, a][:, t * P : (t + 1) * P].bitcast(FP8X4),
+                        lhsT_scale=w1s[b, a][:, t * P : (t + 1) * P],
+                        rhs=vw[a][:, s * BANK : (s + 1) * BANK].bitcast(FP8X4),
+                        rhs_scale=vs[4 * a : P, s * BANK : (s + 1) * BANK],
+                        start=(a == 0),
+                        stop=(a == PASSES - 1),
+                    )
+
+        def rows(b, t):
+            h = ring.tile([P, S], F32, name="h", bufs=5)
+            tops = ring.tile([P, 2], F32, name="tops", bufs=8)
+            ntop = ring.tile([P, 1], F32, name="ntop", bufs=8)
+            for s in range(2):
+                nc.vector.tensor_scalar(
+                    out=h[:, s * BANK : (s + 1) * BANK],
+                    in0=banks[b, t, s][:],
+                    scalar1=1.0,
+                    scalar2=None,
+                    op0=ALU.mult,
+                    op1=ALU.max,
+                    accum_out=tops[:, s : s + 1],
+                )
+            nc.vector.tensor_scalar(
+                out=ntop[:], in0=tops[:, 0:1], scalar1=tops[:, 1:2], scalar2=-1.0, op0=ALU.max, op1=ALU.mult
+            )
+            look[b, t] = keep.tile([P, M], F32, name=f"look{b}{t}")
+            nc.scalar.activation(out=look[b, t][:], in_=h[:].indirect(pos1_sb[:]), func=ACT.Exp, bias=ntop[:])
+            nc.vector.tensor_copy(out=diff[b][:, t, :], in_=h[:].indirect(pos2_sb[:]))
+            nc.vector.scalar_tensor_tensor(
+                out=diff[b][:, t, :],
+                in0=look[b, t][:],
+                scalar=kick_sb[:, b, t : t + 1],
+                in1=diff[b][:, t, :],
+                op0=ALU.mult,
+                op1=ALU.subtract,
+            )
+
+        def scaled_look(b, t):
+            nc.scalar.activation(out=y[b][:, t, :], in_=look[b, t][:], func=ACT.Copy, scale=gain[:, b, t : t + 1])
+
+        def quant_d(b, parts):
+            d_bf = ring.tile([P, M, PACK], BF16, name="packed_bf", bufs=2, align_bytes=64)
+            w = M // parts
+            for u in range(parts):
+                cols = slice(u * w, (u + 1) * w)
+                nc.vector.tensor_tensor(
+                    out=d_bf[:, cols, :].rearrange("p (c q) i -> p c i q", q=4),
+                    in0=diff[b][:, :, cols].rearrange("p i (c q) -> p c i q", q=4),
+                    in1=surf_sb[b][:, :, cols].rearrange("p i (c q) -> p c i q", q=4),
+                    op=ALU.mult,
+                )
+            for u in range(parts):
+                cols = slice(u * w, (u + 1) * w)
+                nc.vector.quantize_mx(
+                    out=d_codes[b][:, cols].bitcast(FP8X4),
+                    scales=d_scales[b][:, cols],
+                    in_=d_bf[:, cols, :].rearrange("p m i -> p (m i)"),
+                )
+
+        nc.vector.memset(tabs[:].bitcast(I32), 0)
+        nc.gpsimd.memset(w4s_raw[:].rearrange("p a n -> p (a n)").bitcast(I32), 0)
+        nc.sync.dma_start(offs_sb[:], offs)
+        load_tab(0)
+        for q in range(4):
+            nc.scalar.dma_start(
+                out=tabs[32 * q : 32 * q + 4 * PASSES, :].bitcast(I32),
+                in_=tab_scales[:, 4 * q : 4 * q + 4, :].bitcast(I32),
+            )
+        load_tab(1)
+        load_w1(0, 0)
+        load_tab(2)
+        for q in range(4):
+            nc.scalar.dma_start(
+                out=w4s_raw[32 * q : 32 * q + 4, :, :].bitcast(I32),
+                in_=w4_scales[:, 4 * q : 4 * q + 4, :].rearrange("a r n -> r a n").bitcast(I32),
+            )
+        load_w1(0, 1)
+        load_w1(0, 2)
+        nc.sync.dma_start(pos1_sb[:], pos1)
+        nc.sync.dma_start(pos2_sb[:], pos2)
+        nc.sync.dma_start(out=kick_sb[:, :, 0:PACK], in_=kick.rearrange("(g p t) -> p g t", g=GROUPS, t=PACK))
+        load_w1(1, 0)
+        load_surf(0)
+
+        for a in range(2):
+            nc.vector.tensor_copy(out=vw[a][:], in_=tabw[a][:].indirect(offs_sb[:]))
+        nc.vector.tensor_copy(out=vs[:], in_=tabs[:].indirect(offs_sb[:]))
+        nc.vector.tensor_copy(out=vw[2][:], in_=tabw[2][:].indirect(offs_sb[:]))
+        for a, share in enumerate((0, 64, 80)):
+            quant_w1(0, a, share)
+            first_product(0, a)
+        load_w1(1, 1)
+        load_w1(1, 2)
+        nc.sync.dma_start(out=span_sb[:, :, 0:PACK], in_=span.rearrange("(g p t) -> p g t", g=GROUPS, t=PACK))
+        nc.sync.dma_start(out=w4w_raw[:].bitcast(I32), in_=w4_words.rearrange("a p c -> p a c").bitcast(I32))
+        load_surf(1)
+        nc.vector.tensor_copy(
+            out=w4s[:].rearrange("p a (g t m) -> p (a g) m t", g=GROUPS, t=PACK),
+            in_=w4s_raw[:].rearrange("p a (g m t) -> p (a g) m t", g=GROUPS, t=PACK),
+        )
+
+        for t in range(PACK):
+            rows(0, t)
+            if t < PASSES:
+                quant_w1(1, t, 0)
+        for a in range(PASSES):
+            first_product(1, a)
+        quant_d(0, 1)
+        nc.vector.tensor_tensor(out=gain[:, :, 0:PACK], in0=kick_sb[:, :, 0:PACK], in1=span_sb[:, :, 0:PACK], op=ALU.mult)
+
+        for t in range(PACK):
+            rows(1, t)
+        nc.scalar.copy(
+            out=w4w[:].rearrange("p a (g t m) -> p (a g) m t", g=GROUPS, t=PACK),
+            in_=w4w_raw[:].rearrange("p a (g m t) -> p (a g) m t", g=GROUPS, t=PACK),
+        )
+        for b in range(GROUPS):
+            for t in range(PACK):
+                scaled_look(b, t)
+        quant_d(1, 2)
+
+        acc = {}
+        for g in range(GROUPS):
+            for t in range(PACK):
+                acc[g, t] = psum.tile([P, BANK], F32, name=f"bank{PACK * g + t}")
+                cols = slice(g * GROUP + t * P, g * GROUP + (t + 1) * P)
+                nc.tensor.matmul_mx(
+                    out=acc[g, t][:],
+                    lhsT=w4w[:, 0, cols].bitcast(FP4X4),
+                    lhsT_scale=w4s[:, 0, cols],
+                    rhs=d_codes[0][:].bitcast(FP8X4),
+                    rhs_scale=d_scales[0][:],
+                    start=True,
+                    stop=False,
+                )
+        for u in range(2):
+            half = slice(u * M // 2, (u + 1) * M // 2)
+            for g in range(GROUPS):
+                for t in range(PACK):
+                    cols = slice(g * GROUP + t * P, g * GROUP + (t + 1) * P)
+                    nc.tensor.matmul_mx(
+                        out=acc[g, t][:, half],
+                        lhsT=w4w[:, 1, cols].bitcast(FP4X4),
+                        lhsT_scale=w4s[:, 1, cols],
+                        rhs=d_codes[1][:, half].bitcast(FP8X4),
+                        rhs_scale=d_scales[1][:, half],
+                        start=False,
+                        stop=(u == 1),
+                    )
+
+        for g, share in enumerate((0, 320)):
+            out_rows = out_0[g * GROUP : (g + 1) * GROUP, :].rearrange("(p t) m -> p t m", t=PACK)
+            for t in range(PACK):
+                nc.vector.scalar_tensor_tensor(
+                    out=y[g][:, t, :],
+                    in0=acc[g, t][:],
+                    scalar=span_sb[:, g, t : t + 1],
+                    in1=y[g][:, t, :],
+                    op0=ALU.mult,
+                    op1=ALU.add,
+                )
+                nc.sync.dma_start(out=out_rows[:, t, :], in_=y[g][:, t, :])
+            y_bf = ring.tile([P, M, PACK], BF16, name="packed_bf", bufs=2, align_bytes=64)
+            dst = y_bf[:].rearrange("p (c q) t -> p c t q", q=4)
+            src = y[g][:].rearrange("p t (c q) -> p c t q", q=4)
+            c0 = share // 4
+            nc.scalar.copy(out=dst[:, c0:], in_=src[:, c0:])
+            if c0 > 0:
+                nc.vector.tensor_copy(out=dst[:, 0:c0], in_=src[:, 0:c0])
+            nc.vector.quantize_mx(
+                out=y_codes[g][:].bitcast(FP8X4), scales=y_scales[:, g, :], in_=y_bf[:].rearrange("p m t -> p (m t)")
+            )
+            nc.sync.dma_start(
+                out=out_1[g].rearrange("p m t -> p (m t)").bitcast(I32), in_=y_codes[g][:].bitcast(I32)
+            )
+        for q in range(4):
+            queue = nc.scalar if q % 2 == 0 else nc.sync
+            queue.dma_start(
+                out=out_2[:, 4 * q : 4 * q + 4, :].rearrange("g r m -> r g m").bitcast(I32),
+                in_=y_scales[32 * q : 32 * q + 4, :, :].bitcast(I32),
+            )

@@ -1,4 +1,5 @@
 from contextlib import ExitStack
+from itertools import product
 
 import concourse.mybir as mybir
 
@@ -40,53 +41,67 @@ def tile_list_stride_asymmetry_features_kernel(
         tabs = keep.tile([P, T], U8, name="tabs", align_bytes=64)
         vw = [keep.tile([P, S], U32, name=f"vw{a}", align_bytes=64) for a in range(PASSES)]
         vs = keep.tile([P, S], U8, name="vs", align_bytes=64)
-        w4s_raw = keep.tile([P, GROUPS, N], U8, name="w4s_raw", align_bytes=64)
-        w4s = keep.tile([P, GROUPS, N], U8, name="w4s", align_bytes=64)
+        w4s_raw = keep.tile([P, N], U8, name="w4s_raw", align_bytes=64)
+        w4s = [keep.tile([P, N], U8, name=f"w4s{a}", align_bytes=64) for a in range(GROUPS)]
         w4w_raw = keep.tile([P, GROUPS, N], U16, name="w4w_raw", align_bytes=64)
         w4w = keep.tile([P, GROUPS, N], U16, name="w4w", align_bytes=64)
         kick_sb = keep.tile([P, GROUPS, 8], F32, name="kick_sb")
         span_sb = keep.tile([P, GROUPS, 8], F32, name="span_sb")
-        gain = keep.tile([P, GROUPS, 8], F32, name="gain")
         surf_sb = [keep.tile([P, PACK, M], F32, name=f"surf{b}") for b in range(GROUPS)]
-        diff = [keep.tile([P, PACK, M], F32, name=f"diff{b}") for b in range(GROUPS)]
-        y = [keep.tile([P, PACK, M], F32, name=f"y{b}") for b in range(GROUPS)]
+        diff = {}
+        stage = [keep.tile([P, PACK, GROUP], F32, name=f"stage{i}") for i in range(3)]
+        last = [keep.tile([P, PACK, GROUP // 2], F32, name=f"last{i}") for i in range(2)]
+        packed = [keep.tile([P, PACK * GROUP], BF16, name=f"packed{i}", align_bytes=64) for i in range(3)]
+        y = {}
+        nspan = keep.tile([P, GROUPS, 8], F32, name="nspan")
         d_codes = [keep.tile([P, M], U32, name=f"d_codes{b}", align_bytes=64) for b in range(GROUPS)]
-        d_scales = [keep.tile([P, M], U8, name=f"d_scales{b}", align_bytes=64) for b in range(GROUPS)]
+        d_scales = {1: keep.tile([P, M], U8, name="d_scales1", align_bytes=64)}
         y_codes = [keep.tile([P, M], U32, name=f"y_codes{b}", align_bytes=64) for b in range(GROUPS)]
         y_scales = keep.tile([P, GROUPS, M], U8, name="y_scales", align_bytes=64)
-        look = {}
+        look, kicked, h = {}, {}, {}
         raw, w1c, w1s, banks = {}, {}, {}, {}
 
         def load_tab(a):
             nc.sync.dma_start(out=tabw[a][:].bitcast(I32), in_=tab_words[a].rearrange("p n i -> p (n i)").bitcast(I32))
 
-        def load_w1(b, a):
-            raw[b, a] = ring.tile([P, PACK, GROUP], F32, name="w1_raw", bufs=4)
-            rows = w1[a * GROUP : (a + 1) * GROUP, b * GROUP : (b + 1) * GROUP]
-            nc.sync.dma_start(out=raw[b, a][:], in_=rows.rearrange("(p j) c -> p j c", j=PACK))
+        def load_w1(b, a, pieces):
+            w = GROUP // len(pieces)
+            raw[b, a] = pieces
+            for u, piece in enumerate(pieces):
+                rows = w1[a * GROUP : (a + 1) * GROUP, b * GROUP + u * w : b * GROUP + (u + 1) * w]
+                nc.sync.dma_start(out=piece[:], in_=rows.rearrange("(p j) c -> p j c", j=PACK))
 
         def load_surf(b):
             nc.sync.dma_start(
                 out=surf_sb[b][:], in_=surf[b * GROUP : (b + 1) * GROUP, :].rearrange("(p i) m -> p i m", i=PACK)
             )
 
-        def quant_w1(b, a, on_vector):
-            grouped = ring.tile([P, PACK, P, PACK], BF16, name="w1_bf", bufs=3, align_bytes=64)
-            dst = grouped[:].rearrange("p t m j -> p m j t")
-            src = raw[b, a][:].rearrange("p j (m t) -> p m j t", t=PACK)
-            if on_vector < P:
-                nc.scalar.copy(out=dst[:, on_vector:P], in_=src[:, on_vector:P])
-            if on_vector > 0:
-                nc.vector.tensor_copy(out=dst[:, 0:on_vector], in_=src[:, 0:on_vector])
+        def cast_w1(b, a, on_vector):
+            flat = packed[a][:]
+            dst = flat.rearrange("p (t m j) -> p m j t", t=PACK, j=PACK)
+            w = P // len(raw[b, a])
+            for u, piece in enumerate(raw[b, a]):
+                src = piece[:].rearrange("p j (m t) -> p m j t", t=PACK)
+                cut = w - on_vector if u == len(raw[b, a]) - 1 else w
+                nc.scalar.copy(out=dst[:, u * w : u * w + cut], in_=src[:, 0:cut])
+                if cut < w:
+                    nc.vector.tensor_copy(out=dst[:, u * w + cut : (u + 1) * w], in_=src[:, cut:w])
+
+        def quant_w1(b, a, parts=1):
+            flat = packed[a][:]
             w1c[b, a] = keep.tile([P, GROUP], U32, name=f"w1c{b}{a}", align_bytes=64)
             w1s[b, a] = keep.tile([P, GROUP], U8, name=f"w1s{b}{a}", align_bytes=64)
-            nc.vector.quantize_mx(
-                out=w1c[b, a][:].bitcast(FP8X4), scales=w1s[b, a][:], in_=grouped[:].rearrange("p t m j -> p (t m j)")
-            )
+            w = GROUP // parts
+            for u in range(parts):
+                nc.vector.quantize_mx(
+                    out=w1c[b, a][:, u * w : (u + 1) * w].bitcast(FP8X4),
+                    scales=w1s[b, a][:, u * w : (u + 1) * w],
+                    in_=flat[:, PACK * u * w : PACK * (u + 1) * w],
+                )
 
-        def first_product(b, a):
+        def first_product(b, passes):
             for t in range(PACK):
-                for s in range(2):
+                for a, s in product(passes, range(2)):
                     if a == 0:
                         banks[b, t, s] = psum.tile([P, BANK], F32, name=f"bank{2 * t + s}")
                     nc.tensor.matmul_mx(
@@ -99,118 +114,151 @@ def tile_list_stride_asymmetry_features_kernel(
                         stop=(a == PASSES - 1),
                     )
 
-        def rows(b, t):
-            h = ring.tile([P, S], F32, name="h", bufs=5)
-            tops = ring.tile([P, 2], F32, name="tops", bufs=8)
+        def empty_banks(b, t):
+            if b == GROUPS - 1 and t >= 1:
+                h[b, t] = ring.tile([P, S], F32, name="h_last", tag=f"late{t}", bufs=1, align_bytes=64)
+            else:
+                h[b, t] = ring.tile([P, S], F32, name="h", bufs=4)
+            tags = (f"kicked{b}{t - 1}" if b > 0 and t > 0 else f"top{b}{t}0", f"diff{b}" if t == PACK - 1 - b else f"top{b}{t}1")
+            tops = [ring.tile([P, 1], F32, name=f"top{s}", tag=tags[s], bufs=1) for s in range(2)]
             ntop = ring.tile([P, 1], F32, name="ntop", bufs=8)
             for s in range(2):
                 nc.vector.tensor_scalar(
-                    out=h[:, s * BANK : (s + 1) * BANK],
+                    out=h[b, t][:, s * BANK : (s + 1) * BANK],
                     in0=banks[b, t, s][:],
                     scalar1=1.0,
                     scalar2=None,
                     op0=ALU.mult,
                     op1=ALU.max,
-                    accum_out=tops[:, s : s + 1],
+                    accum_out=tops[s][:],
                 )
-            nc.vector.tensor_scalar(
-                out=ntop[:], in0=tops[:, 0:1], scalar1=tops[:, 1:2], scalar2=-1.0, op0=ALU.max, op1=ALU.mult
+            nc.gpsimd.tensor_scalar(
+                out=ntop[:], in0=tops[0][:], scalar1=tops[1][:], scalar2=-1.0, op0=ALU.max, op1=ALU.mult
             )
-            look[b, t] = keep.tile([P, M], F32, name=f"look{b}{t}")
-            nc.scalar.activation(out=look[b, t][:], in_=h[:].indirect(pos1_sb[:]), func=ACT.Exp, bias=ntop[:])
-            nc.vector.tensor_copy(out=diff[b][:, t, :], in_=h[:].indirect(pos2_sb[:]))
-            nc.vector.scalar_tensor_tensor(
-                out=diff[b][:, t, :],
-                in0=look[b, t][:],
-                scalar=kick_sb[:, b, t : t + 1],
-                in1=diff[b][:, t, :],
-                op0=ALU.mult,
-                op1=ALU.subtract,
+            look[b, t] = ring.tile([P, M], F32, name="look", bufs=3)
+            nc.scalar.activation(out=look[b, t][:], in_=h[b, t][:].indirect(pos1_sb[:]), func=ACT.Exp, bias=ntop[:])
+
+        def apply_kick(b, t):
+            kicked[b, t] = ring.tile([P, M], F32, name="kicked", tag=f"kicked{b}{t}", bufs=1)
+            nc.scalar.activation(out=kicked[b, t][:], in_=look[b, t][:], func=ACT.Copy, scale=kick_sb[:, b, t : t + 1])
+
+        def pick_fused(b, t):
+            if t == 0:
+                diff[b] = ring.tile([P, PACK, M], F32, name="diff", tag=f"diff{b}", bufs=1)
+            nc.vector.tensor_tensor(
+                out=diff[b][:, t, :], in0=h[b, t][:].indirect(pos2_sb[:]), in1=kicked[b, t][:], op=ALU.subtract
             )
 
-        def scaled_look(b, t):
-            nc.scalar.activation(out=y[b][:, t, :], in_=look[b, t][:], func=ACT.Copy, scale=gain[:, b, t : t + 1])
+        def scaled_look(b, t, factor):
+            nc.scalar.activation(out=y[b][:, t, :], in_=kicked[b, t][:], func=ACT.Copy, scale=factor[:, b, t : t + 1])
 
-        def quant_d(b, parts):
-            d_bf = ring.tile([P, M, PACK], BF16, name="packed_bf", bufs=2, align_bytes=64)
-            w = M // parts
-            for u in range(parts):
-                cols = slice(u * w, (u + 1) * w)
-                nc.vector.tensor_tensor(
-                    out=d_bf[:, cols, :].rearrange("p (c q) i -> p c i q", q=4),
-                    in0=diff[b][:, :, cols].rearrange("p i (c q) -> p c i q", q=4),
-                    in1=surf_sb[b][:, :, cols].rearrange("p i (c q) -> p c i q", q=4),
-                    op=ALU.mult,
-                )
-            for u in range(parts):
-                cols = slice(u * w, (u + 1) * w)
-                nc.vector.quantize_mx(
-                    out=d_codes[b][:, cols].bitcast(FP8X4),
-                    scales=d_scales[b][:, cols],
-                    in_=d_bf[:, cols, :].rearrange("p m i -> p (m i)"),
-                )
+        def weigh_d(b, u):
+            w = M // 2
+            cols = slice(u * w, (u + 1) * w)
+            d_bf = packed[1 + u][:, b * PACK * w : (b + 1) * PACK * w]
+            nc.vector.tensor_tensor(
+                out=d_bf.rearrange("p (c q i) -> p c i q", q=4, i=PACK),
+                in0=diff[b][:, :, cols].rearrange("p i (c q) -> p c i q", q=4),
+                in1=surf_sb[b][:, :, cols].rearrange("p i (c q) -> p c i q", q=4),
+                op=ALU.mult,
+            )
+
+        def quant_d(b, u):
+            w = M // 2
+            cols = slice(u * w, (u + 1) * w)
+            d_bf = packed[1 + u][:, b * PACK * w : (b + 1) * PACK * w]
+            nc.vector.quantize_mx(out=d_codes[b][:, cols].bitcast(FP8X4), scales=d_scales[b][:, cols], in_=d_bf)
 
         nc.vector.memset(tabs[:].bitcast(I32), 0)
-        nc.gpsimd.memset(w4s_raw[:].rearrange("p a n -> p (a n)").bitcast(I32), 0)
+        nc.gpsimd.memset(w4s_raw[:].bitcast(I32), 0)
+        nc.gpsimd.memset(w4s[1][:].bitcast(I32), 0)
         nc.sync.dma_start(offs_sb[:], offs)
         load_tab(0)
+        load_w1(0, 0, [stage[0]])
         for q in range(4):
-            nc.scalar.dma_start(
+            nc.sync.dma_start(
                 out=tabs[32 * q : 32 * q + 4 * PASSES, :].bitcast(I32),
                 in_=tab_scales[:, 4 * q : 4 * q + 4, :].bitcast(I32),
             )
         load_tab(1)
-        load_w1(0, 0)
+        load_w1(0, 1, [stage[1]])
         load_tab(2)
-        for q in range(4):
-            nc.scalar.dma_start(
-                out=w4s_raw[32 * q : 32 * q + 4, :, :].bitcast(I32),
-                in_=w4_scales[:, 4 * q : 4 * q + 4, :].rearrange("a r n -> r a n").bitcast(I32),
-            )
-        load_w1(0, 1)
-        load_w1(0, 2)
+        load_w1(0, 2, last)
         nc.sync.dma_start(pos1_sb[:], pos1)
         nc.sync.dma_start(pos2_sb[:], pos2)
+        load_w1(1, 0, [stage[2]])
         nc.sync.dma_start(out=kick_sb[:, :, 0:PACK], in_=kick.rearrange("(g p t) -> p g t", g=GROUPS, t=PACK))
-        load_w1(1, 0)
-        load_surf(0)
 
-        for a in range(2):
-            nc.vector.tensor_copy(out=vw[a][:], in_=tabw[a][:].indirect(offs_sb[:]))
+        nc.vector.tensor_copy(out=vw[0][:], in_=tabw[0][:].indirect(offs_sb[:]))
         nc.vector.tensor_copy(out=vs[:], in_=tabs[:].indirect(offs_sb[:]))
-        nc.vector.tensor_copy(out=vw[2][:], in_=tabw[2][:].indirect(offs_sb[:]))
-        for a, share in enumerate((0, 64, 80)):
-            quant_w1(0, a, share)
-            first_product(0, a)
-        load_w1(1, 1)
-        load_w1(1, 2)
-        nc.sync.dma_start(out=span_sb[:, :, 0:PACK], in_=span.rearrange("(g p t) -> p g t", g=GROUPS, t=PACK))
-        nc.sync.dma_start(out=w4w_raw[:].bitcast(I32), in_=w4_words.rearrange("a p c -> p a c").bitcast(I32))
+        for a, share in enumerate((0, 40, 40)):
+            if a > 0:
+                nc.vector.tensor_copy(out=vw[a][:], in_=tabw[a][:].indirect(offs_sb[:]))
+            cast_w1(0, a, share)
+            quant_w1(0, a, 2 if a == PASSES - 1 else 1)
+            first_product(0, [a])
+        load_w1(1, 1, [stage[0]])
+        for q in range(4):
+            nc.sync.dma_start(
+                out=w4s_raw[32 * q : 32 * q + 4 * GROUPS, :].bitcast(I32),
+                in_=w4_scales[:, 4 * q : 4 * q + 4, :].bitcast(I32),
+            )
+        load_w1(1, 2, [stage[1]])
+        load_surf(0)
         load_surf(1)
+        nc.sync.dma_start(out=w4w_raw[:].bitcast(I32), in_=w4_words.rearrange("a p c -> p a c").bitcast(I32))
+        nc.sync.dma_start(out=span_sb[:, :, 0:PACK], in_=span.rearrange("(g p t) -> p g t", g=GROUPS, t=PACK))
+
+        cast_w1(1, 0, 0)
+        for t in range(PACK):
+            empty_banks(0, t)
+            apply_kick(0, t)
+        quant_w1(1, 0)
+        first_product(1, [0])
+        cast_w1(1, 1, 48)
         nc.vector.tensor_copy(
-            out=w4s[:].rearrange("p a (g t m) -> p (a g) m t", g=GROUPS, t=PACK),
-            in_=w4s_raw[:].rearrange("p a (g m t) -> p (a g) m t", g=GROUPS, t=PACK),
+            out=w4s[0][:].rearrange("p (g t m) -> p g t m", g=GROUPS, t=PACK),
+            in_=w4s_raw[:].rearrange("p (g m t) -> p g t m", g=GROUPS, t=PACK),
         )
-
+        for q in range(4):
+            nc.sync.dma_start(
+                out=w4s[1][32 * q : 32 * q + 4, :].bitcast(I32), in_=w4s[0][32 * q + 4 : 32 * q + 8, :].bitcast(I32)
+            )
         for t in range(PACK):
-            rows(0, t)
-            if t < PASSES:
-                quant_w1(1, t, 0)
-        for a in range(PASSES):
-            first_product(1, a)
-        quant_d(0, 1)
-        nc.vector.tensor_tensor(out=gain[:, :, 0:PACK], in0=kick_sb[:, :, 0:PACK], in1=span_sb[:, :, 0:PACK], op=ALU.mult)
-
-        for t in range(PACK):
-            rows(1, t)
+            pick_fused(0, t)
+        quant_w1(1, 1)
+        cast_w1(1, 2, 0)
+        weigh_d(0, 0)
+        quant_w1(1, 2)
+        first_product(1, [1, 2])
+        weigh_d(0, 1)
+        nc.gpsimd.tensor_scalar(
+            out=nspan[:, :, 0:PACK], in0=span_sb[:, :, 0:PACK], scalar1=-1.0, scalar2=0.0, op0=ALU.mult, op1=ALU.add
+        )
         nc.scalar.copy(
-            out=w4w[:].rearrange("p a (g t m) -> p (a g) m t", g=GROUPS, t=PACK),
-            in_=w4w_raw[:].rearrange("p a (g m t) -> p (a g) m t", g=GROUPS, t=PACK),
+            out=w4w[:].rearrange("p a (g t m) -> p (a g) t m", g=GROUPS, t=PACK),
+            in_=w4w_raw[:].rearrange("p a (g m t) -> p (a g) t m", g=GROUPS, t=PACK),
         )
+
+        for t in range(PACK):
+            empty_banks(1, t)
+            if t > 0:
+                apply_kick(1, t - 1)
+        apply_kick(1, PACK - 1)
+        for t in range(PACK):
+            pick_fused(1, t)
+            if t == 1:
+                d_scales[0] = ring.tile([P, M], U8, name="d_scales0", tag="late1", bufs=1, align_bytes=64)
+                for u in range(2):
+                    quant_d(0, u)
         for b in range(GROUPS):
+            y[b] = ring.tile([P, PACK, M], F32, name="y", tag=f"late{PACK - GROUPS + b}", bufs=1, align_bytes=64)
             for t in range(PACK):
-                scaled_look(b, t)
-        quant_d(1, 2)
+                scaled_look(b, t, span_sb)
+        for u in range(2):
+            weigh_d(1, u)
+        for u in range(2):
+            quant_d(1, u)
 
         acc = {}
         for g in range(GROUPS):
@@ -220,52 +268,60 @@ def tile_list_stride_asymmetry_features_kernel(
                 nc.tensor.matmul_mx(
                     out=acc[g, t][:],
                     lhsT=w4w[:, 0, cols].bitcast(FP4X4),
-                    lhsT_scale=w4s[:, 0, cols],
+                    lhsT_scale=w4s[0][:, cols],
                     rhs=d_codes[0][:].bitcast(FP8X4),
                     rhs_scale=d_scales[0][:],
                     start=True,
                     stop=False,
                 )
-        for u in range(2):
-            half = slice(u * M // 2, (u + 1) * M // 2)
-            for g in range(GROUPS):
-                for t in range(PACK):
+        for g in range(GROUPS):
+            for t in range(PACK):
+                for u in range(2):
+                    half = slice(u * M // 2, (u + 1) * M // 2)
                     cols = slice(g * GROUP + t * P, g * GROUP + (t + 1) * P)
                     nc.tensor.matmul_mx(
                         out=acc[g, t][:, half],
                         lhsT=w4w[:, 1, cols].bitcast(FP4X4),
-                        lhsT_scale=w4s[:, 1, cols],
+                        lhsT_scale=w4s[1][:, cols],
                         rhs=d_codes[1][:, half].bitcast(FP8X4),
                         rhs_scale=d_scales[1][:, half],
                         start=False,
                         stop=(u == 1),
                     )
 
-        for g, share in enumerate((0, 320)):
+        def finish_rows(g):
             out_rows = out_0[g * GROUP : (g + 1) * GROUP, :].rearrange("(p t) m -> p t m", t=PACK)
             for t in range(PACK):
                 nc.vector.scalar_tensor_tensor(
                     out=y[g][:, t, :],
                     in0=acc[g, t][:],
-                    scalar=span_sb[:, g, t : t + 1],
+                    scalar=nspan[:, g, t : t + 1],
                     in1=y[g][:, t, :],
                     op0=ALU.mult,
                     op1=ALU.add,
                 )
                 nc.sync.dma_start(out=out_rows[:, t, :], in_=y[g][:, t, :])
-            y_bf = ring.tile([P, M, PACK], BF16, name="packed_bf", bufs=2, align_bytes=64)
-            dst = y_bf[:].rearrange("p (c q) t -> p c t q", q=4)
+
+        def round_y(g, on_vector):
+            dst = packed[g][:].rearrange("p (c q t) -> p c t q", q=4, t=PACK)
             src = y[g][:].rearrange("p t (c q) -> p c t q", q=4)
-            c0 = share // 4
+            c0 = on_vector // 4
             nc.scalar.copy(out=dst[:, c0:], in_=src[:, c0:])
             if c0 > 0:
                 nc.vector.tensor_copy(out=dst[:, 0:c0], in_=src[:, 0:c0])
-            nc.vector.quantize_mx(
-                out=y_codes[g][:].bitcast(FP8X4), scales=y_scales[:, g, :], in_=y_bf[:].rearrange("p m t -> p (m t)")
-            )
+
+        def quant_y(g):
+            nc.vector.quantize_mx(out=y_codes[g][:].bitcast(FP8X4), scales=y_scales[:, g, :], in_=packed[g][:])
             nc.sync.dma_start(
                 out=out_1[g].rearrange("p m t -> p (m t)").bitcast(I32), in_=y_codes[g][:].bitcast(I32)
             )
+
+        finish_rows(0)
+        round_y(0, 0)
+        finish_rows(1)
+        quant_y(0)
+        round_y(1, 288)
+        quant_y(1)
         for q in range(4):
             queue = nc.scalar if q % 2 == 0 else nc.sync
             queue.dma_start(

@@ -83,7 +83,8 @@ def tile_list_stride_asymmetry_features_kernel(
             for u, piece in enumerate(raw[b, a]):
                 src = piece[:].rearrange("p j (m t) -> p m j t", t=PACK)
                 cut = w - on_vector if u == len(raw[b, a]) - 1 else w
-                nc.scalar.copy(out=dst[:, u * w : u * w + cut], in_=src[:, 0:cut])
+                if cut > 0:
+                    nc.scalar.copy(out=dst[:, u * w : u * w + cut], in_=src[:, 0:cut])
                 if cut < w:
                     nc.vector.tensor_copy(out=dst[:, u * w + cut : (u + 1) * w], in_=src[:, cut:w])
 
@@ -215,7 +216,7 @@ def tile_list_stride_asymmetry_features_kernel(
             apply_kick(0, t)
         quant_w1(1, 0)
         first_product(1, [0])
-        cast_w1(1, 1, 48)
+        cast_w1(1, 1, P)
         nc.vector.tensor_copy(
             out=w4s[0][:].rearrange("p (g t m) -> p g t m", g=GROUPS, t=PACK),
             in_=w4s_raw[:].rearrange("p (g m t) -> p g t m", g=GROUPS, t=PACK),

from contextlib import ExitStack
from itertools import product

import concourse.mybir as mybir

K, T, S, M, H, N = 1536, 2048, 1024, 512, 1024, 1024
FLOPS = 2 * K * H * S + 2 * H * N * M

F32 = mybir.dt.float32
BF16 = mybir.dt.bfloat16
I32 = mybir.dt.int32
U32 = mybir.dt.uint32
U16 = mybir.dt.uint16
U8 = mybir.dt.uint8
FP8X4 = mybir.dt.float8_e4m3fn_x4
FP4X4 = mybir.dt.float4_e2m1fn_x4
ALU = mybir.AluOpType
ACT = mybir.ActivationFunctionType

P = 128
PACK = 4
GROUP = P * PACK
PASSES = K // GROUP
GROUPS = H // GROUP
BANK = 512


def tile_list_stride_asymmetry_features_kernel(
    tc, tab_words, tab_scales, offs, pos1, pos2, w1, kick, surf, w4_words, w4_scales, span, out_0, out_1, out_2
):
    nc = tc.nc
    with ExitStack() as ctx:
        keep = ctx.enter_context(tc.tile_pool(name="keep", bufs=1))
        ring = ctx.enter_context(tc.tile_pool(name="ring", bufs=1))
        psum = ctx.enter_context(tc.psum_pool(name="psum", bufs=1))

        offs_sb = keep.tile([P, S // 16], U16, name="offs_sb")
        pos1_sb = keep.tile([P, M // 16], U16, name="pos1_sb")
        pos2_sb = keep.tile([P, M // 16], U16, name="pos2_sb")
        tabw = [keep.tile([P, T], U32, name=f"tabw{a}", align_bytes=64) for a in range(PASSES)]
        tabs = keep.tile([P, T], U8, name="tabs", align_bytes=64)
        vw = [keep.tile([P, S], U32, name=f"vw{a}", align_bytes=64) for a in range(PASSES)]
        vs = keep.tile([P, S], U8, name="vs", align_bytes=64)
        w4s_raw = keep.tile([P, N], U8, name="w4s_raw", align_bytes=64)
        w4s = [keep.tile([P, N], U8, name=f"w4s{a}", align_bytes=64) for a in range(GROUPS)]
        w4w_raw = keep.tile([P, GROUPS, N], U16, name="w4w_raw", align_bytes=64)
        w4w = keep.tile([P, GROUPS, N], U16, name="w4w", align_bytes=64)
        kick_sb = keep.tile([P, GROUPS, 8], F32, name="kick_sb")
        span_sb = keep.tile([P, GROUPS, 8], F32, name="span_sb")
        surf_sb = [keep.tile([P, PACK, M], F32, name=f"surf{b}") for b in range(GROUPS)]
        diff = {}
        stage = [keep.tile([P, PACK, GROUP], F32, name=f"stage{i}") for i in range(3)]
        last = [keep.tile([P, PACK, GROUP // 2], F32, name=f"last{i}") for i in range(2)]
        packed = [keep.tile([P, PACK * GROUP], BF16, name=f"packed{i}", align_bytes=64) for i in range(3)]
        y = {}
        nspan = keep.tile([P, GROUPS, 8], F32, name="nspan")
        d_codes = [keep.tile([P, M], U32, name=f"d_codes{b}", align_bytes=64) for b in range(GROUPS)]
        d_scales = {1: keep.tile([P, M], U8, name="d_scales1", align_bytes=64)}
        y_codes = [keep.tile([P, M], U32, name=f"y_codes{b}", align_bytes=64) for b in range(GROUPS)]
        y_scales = keep.tile([P, GROUPS, M], U8, name="y_scales", align_bytes=64)
        look, kicked, h = {}, {}, {}
        raw, w1c, w1s, banks = {}, {}, {}, {}

        def load_tab(a):
            nc.sync.dma_start(out=tabw[a][:].bitcast(I32), in_=tab_words[a].rearrange("p n i -> p (n i)").bitcast(I32))

        def load_w1(b, a, pieces):
            w = GROUP // len(pieces)
            raw[b, a] = pieces
            for u, piece in enumerate(pieces):
                rows = w1[a * GROUP : (a + 1) * GROUP, b * GROUP + u * w : b * GROUP + (u + 1) * w]
                nc.sync.dma_start(out=piece[:], in_=rows.rearrange("(p j) c -> p j c", j=PACK))

        def load_surf(b):
            nc.sync.dma_start(
                out=surf_sb[b][:], in_=surf[b * GROUP : (b + 1) * GROUP, :].rearrange("(p i) m -> p i m", i=PACK)
            )

        def cast_w1(b, a, on_vector):
            flat = packed[a][:]
            dst = flat.rearrange("p (t m j) -> p m j t", t=PACK, j=PACK)
            w = P // len(raw[b, a])
            for u, piece in enumerate(raw[b, a]):
                src = piece[:].rearrange("p j (m t) -> p m j t", t=PACK)
                cut = w - on_vector if u == len(raw[b, a]) - 1 else w
                if cut > 0:
                    nc.scalar.copy(out=dst[:, u * w : u * w + cut], in_=src[:, 0:cut])
                if cut < w:
                    nc.vector.tensor_copy(out=dst[:, u * w + cut : (u + 1) * w], in_=src[:, cut:w])

        def quant_w1(b, a, parts=1):
            flat = packed[a][:]
            w1c[b, a] = keep.tile([P, GROUP], U32, name=f"w1c{b}{a}", align_bytes=64)
            w1s[b, a] = keep.tile([P, GROUP], U8, name=f"w1s{b}{a}", align_bytes=64)
            w = GROUP // parts
            for u in range(parts):
                nc.vector.quantize_mx(
                    out=w1c[b, a][:, u * w : (u + 1) * w].bitcast(FP8X4),
                    scales=w1s[b, a][:, u * w : (u + 1) * w],
                    in_=flat[:, PACK * u * w : PACK * (u + 1) * w],
                )

        def first_product(b, passes):
            for t in range(PACK):
                for a, s in product(passes, range(2)):
                    if a == 0:
                        banks[b, t, s] = psum.tile([P, BANK], F32, name=f"bank{2 * t + s}")
                    nc.tensor.matmul_mx(
                        out=banks[b, t, s][:],
                        lhsT=w1c[b, a][:, t * P : (t + 1) * P].bitcast(FP8X4),
                        lhsT_scale=w1s[b, a][:, t * P : (t + 1) * P],
                        rhs=vw[a][:, s * BANK : (s + 1) * BANK].bitcast(FP8X4),
                        rhs_scale=vs[4 * a : P, s * BANK : (s + 1) * BANK],
                        start=(a == 0),
                        stop=(a == PASSES - 1),
                    )

        def empty_banks(b, t):
            if b == GROUPS - 1 and t >= 1:
                h[b, t] = ring.tile([P, S], F32, name="h_last", tag=f"late{t}", bufs=1, align_bytes=64)
            else:
                h[b, t] = ring.tile([P, S], F32, name="h", bufs=4)
            tags = (f"kicked{b}{t - 1}" if b > 0 and t > 0 else f"top{b}{t}0", f"diff{b}" if t == PACK - 1 - b else f"top{b}{t}1")
            tops = [ring.tile([P, 1], F32, name=f"top{s}", tag=tags[s], bufs=1) for s in range(2)]
            ntop = ring.tile([P, 1], F32, name="ntop", bufs=8)
            for s in range(2):
                nc.vector.tensor_scalar(
                    out=h[b, t][:, s * BANK : (s + 1) * BANK],
                    in0=banks[b, t, s][:],
                    scalar1=1.0,
                    scalar2=None,
                    op0=ALU.mult,
                    op1=ALU.max,
                    accum_out=tops[s][:],
                )
            nc.gpsimd.tensor_scalar(
                out=ntop[:], in0=tops[0][:], scalar1=tops[1][:], scalar2=-1.0, op0=ALU.max, op1=ALU.mult
            )
            look[b, t] = ring.tile([P, M], F32, name="look", bufs=3)
            nc.scalar.activation(out=look[b, t][:], in_=h[b, t][:].indirect(pos1_sb[:]), func=ACT.Exp, bias=ntop[:])

        def apply_kick(b, t):
            kicked[b, t] = ring.tile([P, M], F32, name="kicked", tag=f"kicked{b}{t}", bufs=1)
            nc.scalar.activation(out=kicked[b, t][:], in_=look[b, t][:], func=ACT.Copy, scale=kick_sb[:, b, t : t + 1])

        def pick_fused(b, t):
            if t == 0:
                diff[b] = ring.tile([P, PACK, M], F32, name="diff", tag=f"diff{b}", bufs=1)
            nc.vector.tensor_tensor(
                out=diff[b][:, t, :], in0=h[b, t][:].indirect(pos2_sb[:]), in1=kicked[b, t][:], op=ALU.subtract
            )

        def scaled_look(b, t, factor):
            nc.scalar.activation(out=y[b][:, t, :], in_=kicked[b, t][:], func=ACT.Copy, scale=factor[:, b, t : t + 1])

        def weigh_d(b, u):
            w = M // 2
            cols = slice(u * w, (u + 1) * w)
            d_bf = packed[1 + u][:, b * PACK * w : (b + 1) * PACK * w]
            nc.vector.tensor_tensor(
                out=d_bf.rearrange("p (c q i) -> p c i q", q=4, i=PACK),
                in0=diff[b][:, :, cols].rearrange("p i (c q) -> p c i q", q=4),
                in1=surf_sb[b][:, :, cols].rearrange("p i (c q) -> p c i q", q=4),
                op=ALU.mult,
            )

        def quant_d(b, u):
            w = M // 2
            cols = slice(u * w, (u + 1) * w)
            d_bf = packed[1 + u][:, b * PACK * w : (b + 1) * PACK * w]
            nc.vector.quantize_mx(out=d_codes[b][:, cols].bitcast(FP8X4), scales=d_scales[b][:, cols], in_=d_bf)

        nc.vector.memset(tabs[:].bitcast(I32), 0)
        nc.gpsimd.memset(w4s_raw[:].bitcast(I32), 0)
        nc.gpsimd.memset(w4s[1][:].bitcast(I32), 0)
        nc.sync.dma_start(offs_sb[:], offs)
        load_tab(0)
        load_w1(0, 0, [stage[0]])
        for q in range(4):
            nc.sync.dma_start(
                out=tabs[32 * q : 32 * q + 4 * PASSES, :].bitcast(I32),
                in_=tab_scales[:, 4 * q : 4 * q + 4, :].bitcast(I32),
            )
        load_tab(1)
        load_w1(0, 1, [stage[1]])
        load_tab(2)
        load_w1(0, 2, last)
        nc.sync.dma_start(pos1_sb[:], pos1)
        nc.sync.dma_start(pos2_sb[:], pos2)
        load_w1(1, 0, [stage[2]])
        nc.sync.dma_start(out=kick_sb[:, :, 0:PACK], in_=kick.rearrange("(g p t) -> p g t", g=GROUPS, t=PACK))

        nc.vector.tensor_copy(out=vw[0][:], in_=tabw[0][:].indirect(offs_sb[:]))
        nc.vector.tensor_copy(out=vs[:], in_=tabs[:].indirect(offs_sb[:]))
        for a, share in enumerate((0, 40, 40)):
            if a > 0:
                nc.vector.tensor_copy(out=vw[a][:], in_=tabw[a][:].indirect(offs_sb[:]))
            cast_w1(0, a, share)
            quant_w1(0, a, 2 if a == PASSES - 1 else 1)
            first_product(0, [a])
        load_w1(1, 1, [stage[0]])
        for q in range(4):
            nc.sync.dma_start(
                out=w4s_raw[32 * q : 32 * q + 4 * GROUPS, :].bitcast(I32),
                in_=w4_scales[:, 4 * q : 4 * q + 4, :].bitcast(I32),
            )
        load_w1(1, 2, [stage[1]])
        load_surf(0)
        load_surf(1)
        nc.sync.dma_start(out=w4w_raw[:].bitcast(I32), in_=w4_words.rearrange("a p c -> p a c").bitcast(I32))
        nc.sync.dma_start(out=span_sb[:, :, 0:PACK], in_=span.rearrange("(g p t) -> p g t", g=GROUPS, t=PACK))

        cast_w1(1, 0, 0)
        for t in range(PACK):
            empty_banks(0, t)
            apply_kick(0, t)
        quant_w1(1, 0)
        first_product(1, [0])
        cast_w1(1, 1, P)
        nc.vector.tensor_copy(
            out=w4s[0][:].rearrange("p (g t m) -> p g t m", g=GROUPS, t=PACK),
            in_=w4s_raw[:].rearrange("p (g m t) -> p g t m", g=GROUPS, t=PACK),
        )
        for q in range(4):
            nc.sync.dma_start(
                out=w4s[1][32 * q : 32 * q + 4, :].bitcast(I32), in_=w4s[0][32 * q + 4 : 32 * q + 8, :].bitcast(I32)
            )
        for t in range(PACK):
            pick_fused(0, t)
        quant_w1(1, 1)
        cast_w1(1, 2, 0)
        weigh_d(0, 0)
        quant_w1(1, 2)
        first_product(1, [1, 2])
        weigh_d(0, 1)
        nc.gpsimd.tensor_scalar(
            out=nspan[:, :, 0:PACK], in0=span_sb[:, :, 0:PACK], scalar1=-1.0, scalar2=0.0, op0=ALU.mult, op1=ALU.add
        )
        nc.scalar.copy(
            out=w4w[:].rearrange("p a (g t m) -> p (a g) t m", g=GROUPS, t=PACK),
            in_=w4w_raw[:].rearrange("p a (g m t) -> p (a g) t m", g=GROUPS, t=PACK),
        )

        for t in range(PACK):
            empty_banks(1, t)
            if t > 0:
                apply_kick(1, t - 1)
        apply_kick(1, PACK - 1)
        for t in range(PACK):
            pick_fused(1, t)
            if t == 1:
                d_scales[0] = ring.tile([P, M], U8, name="d_scales0", tag="late1", bufs=1, align_bytes=64)
                for u in range(2):
                    quant_d(0, u)
        for b in range(GROUPS):
            y[b] = ring.tile([P, PACK, M], F32, name="y", tag=f"late{PACK - GROUPS + b}", bufs=1, align_bytes=64)
            for t in range(PACK):
                scaled_look(b, t, span_sb)
        for u in range(2):
            weigh_d(1, u)
        for u in range(2):
            quant_d(1, u)

        acc = {}
        for g in range(GROUPS):
            for t in range(PACK):
                acc[g, t] = psum.tile([P, BANK], F32, name=f"bank{PACK * g + t}")
                cols = slice(g * GROUP + t * P, g * GROUP + (t + 1) * P)
                nc.tensor.matmul_mx(
                    out=acc[g, t][:],
                    lhsT=w4w[:, 0, cols].bitcast(FP4X4),
                    lhsT_scale=w4s[0][:, cols],
                    rhs=d_codes[0][:].bitcast(FP8X4),
                    rhs_scale=d_scales[0][:],
                    start=True,
                    stop=False,
                )
        for g in range(GROUPS):
            for t in range(PACK):
                for u in range(2):
                    half = slice(u * M // 2, (u + 1) * M // 2)
                    cols = slice(g * GROUP + t * P, g * GROUP + (t + 1) * P)
                    nc.tensor.matmul_mx(
                        out=acc[g, t][:, half],
                        lhsT=w4w[:, 1, cols].bitcast(FP4X4),
                        lhsT_scale=w4s[1][:, cols],
                        rhs=d_codes[1][:, half].bitcast(FP8X4),
                        rhs_scale=d_scales[1][:, half],
                        start=False,
                        stop=(u == 1),
                    )

        def finish_rows(g):
            out_rows = out_0[g * GROUP : (g + 1) * GROUP, :].rearrange("(p t) m -> p t m", t=PACK)
            for t in range(PACK):
                nc.vector.scalar_tensor_tensor(
                    out=y[g][:, t, :],
                    in0=acc[g, t][:],
                    scalar=nspan[:, g, t : t + 1],
                    in1=y[g][:, t, :],
                    op0=ALU.mult,
                    op1=ALU.add,
                )
                nc.sync.dma_start(out=out_rows[:, t, :], in_=y[g][:, t, :])

        def round_y(g, on_vector):
            dst = packed[g][:].rearrange("p (c q t) -> p c t q", q=4, t=PACK)
            src = y[g][:].rearrange("p t (c q) -> p c t q", q=4)
            c0 = on_vector // 4
            nc.scalar.copy(out=dst[:, c0:], in_=src[:, c0:])
            if c0 > 0:
                nc.vector.tensor_copy(out=dst[:, 0:c0], in_=src[:, 0:c0])

        def quant_y(g):
            nc.vector.quantize_mx(out=y_codes[g][:].bitcast(FP8X4), scales=y_scales[:, g, :], in_=packed[g][:])
            nc.sync.dma_start(
                out=out_1[g].rearrange("p m t -> p (m t)").bitcast(I32), in_=y_codes[g][:].bitcast(I32)
            )

        finish_rows(0)
        round_y(0, 0)
        finish_rows(1)
        quant_y(0)
        round_y(1, 288)
        quant_y(1)
        for q in range(4):
            queue = nc.scalar if q % 2 == 0 else nc.sync
            queue.dma_start(
                out=out_2[:, 4 * q : 4 * q + 4, :].rearrange("g r m -> r g m").bitcast(I32),
                in_=y_scales[32 * q : 32 * q + 4, :, :].bitcast(I32),
            )
